import numpy as np
import ml_dtypes


def mxq(x, axis, fmt="e4m3"):
    dtype, down = {"e4m3": (ml_dtypes.float8_e4m3fn, 7), "e5m2": (ml_dtypes.float8_e5m2, 14)}[fmt]
    v = np.moveaxis(np.asarray(x, np.float32).astype(ml_dtypes.bfloat16).astype(np.float64), axis, -1)
    blocks = v.reshape(v.shape[:-1] + (-1, 32))
    amax = np.abs(blocks).max(-1, keepdims=True)
    byte = np.maximum(np.where(amax > 0, np.frexp(amax)[1] - 1 + 127, 0) - down, 1)
    scale = np.exp2(byte - 127.0)
    codes = (blocks / scale).astype(np.float32).astype(dtype).astype(np.float64)
    return np.moveaxis((codes * scale).reshape(v.shape), -1, axis)


WIDE = False


def mx_kscale(k):
    if not WIDE:
        return np.ones(k)
    levels = np.array([10, -10, 5, -5, 0])
    if k % 512:
        return np.exp2(np.random.permutation(np.resize(levels, k // 32))).repeat(32)
    a = np.empty((k // 512, 16))
    for p in range(k // 512):
        a[p, :8] = np.random.permutation(np.resize(levels, 8))
        for g in range(8):
            far = levels[np.abs(levels - a[p, g]) >= 10]
            a[p, g + 8] = far[np.random.randint(len(far))]
    return np.exp2(a.ravel()).repeat(32)


def f64(x):
    return np.asarray(x).astype(np.float64)


def striped(idx):
    return np.tile(idx.reshape(-1, 16).T, (8, 1)).astype(np.uint16)


def unstriped(offs):
    return offs[:16].T.reshape(-1).astype(np.int64)


def striped8(idx):
    return np.concatenate([x.reshape(-1, 16).T for x in idx]).astype(np.uint16)


def runs(offs, k):
    lists = np.stack([offs[16 * r : 16 * r + 16].T.reshape(-1) for r in range(8)]).astype(np.int64)
    return lists[np.arange(k) % 512 // 64]


def pack_weight(w):
    k, n = w.shape
    w = f64(np.asarray(w, np.float32).astype(ml_dtypes.bfloat16)).reshape(k // 32, 32, n)
    amax = np.abs(w).max(1)
    byte = np.clip(np.where(amax > 0, np.frexp(amax)[1] - 1 + 127 - 7, 1), 1, 254)
    scaled = (w * np.exp2(127.0 - byte)[:, None, :]).reshape(k, n).astype(np.float32)
    words = np.ascontiguousarray(scaled.reshape(k // 512, 128, 4, n).transpose(0, 1, 3, 2)).astype(ml_dtypes.float8_e4m3fn).view(np.uint8)
    return words, np.ascontiguousarray(byte.astype(np.uint8).reshape(k // 512, 16, n))


def unpack_weight(words, scales):
    g, p, n, _ = words.shape
    vals = np.ascontiguousarray(words).view(ml_dtypes.float8_e4m3fn).astype(np.float64) * np.repeat(np.exp2(scales.astype(np.float64) - 127.0), 8, axis=1)[..., None]
    return vals.transpose(0, 1, 3, 2).reshape(g * 512, n)


E2M1 = np.array([0.0, 0.5, 1.0, 1.5, 2.0, 3.0, 4.0, 6.0, -0.0, -0.5, -1.0, -1.5, -2.0, -3.0, -4.0, -6.0])


def pack_fp4(w):
    k, n = w.shape
    w = f64(np.asarray(w, np.float32).astype(ml_dtypes.bfloat16)).reshape(k // 32, 32, n)
    amax = np.abs(w).max(1)
    mant, ex = np.frexp(amax / 6.0)
    byte = np.clip(np.where(amax > 0, np.where(mant > 0.5, ex, ex - 1) + 127, 1), 1, 254)
    scaled = (w * np.exp2(127.0 - byte)[:, None, :]).reshape(k, n).astype(np.float32)
    c = np.ascontiguousarray(scaled.reshape(k // 512, 128, 4, n).transpose(0, 1, 3, 2)).astype(ml_dtypes.float4_e2m1fn).view(np.uint8) & 0xF
    words = (c[..., 0::2] | (c[..., 1::2] << 4)).reshape(k // 512, 128, 2 * n)
    return np.ascontiguousarray(words), np.ascontiguousarray(byte.astype(np.uint8).reshape(k // 512, 16, n))


def unpack_fp4(words, scales):
    g, _, n = scales.shape
    words = np.ascontiguousarray(words).reshape(g, 128, n, 2)
    nib = np.empty((g, 128, n, 4), np.uint8)
    nib[..., 0::2] = words & 0xF
    nib[..., 1::2] = words >> 4
    vals = E2M1[nib] * np.repeat(np.exp2(scales.astype(np.float64) - 127.0), 8, axis=1)[..., None]
    return vals.transpose(0, 1, 3, 2).reshape(g * 512, n)


def sigmoid(v):
    return 1.0 / (1.0 + np.exp(-np.maximum(v, -700.0)))

def planes(y):
    n, m = y.shape
    v = y.astype(np.float32).astype(ml_dtypes.bfloat16).astype(np.float64).reshape(n // 32, 32, m)
    top = np.abs(v).max(1)
    byte = np.clip(np.where(top > 0, np.frexp(top)[1] - 1 + 127 - 7, 1), 1, 254)
    codes = (v * np.exp2(127.0 - byte)[:, None, :]).reshape(n, m).astype(np.float32).astype(ml_dtypes.float8_e4m3fn).view(np.uint8)
    words = codes.reshape(n // 512, 128, 4, m).transpose(0, 1, 3, 2)
    return np.ascontiguousarray(words), np.ascontiguousarray(byte.astype(np.uint8).reshape(n // 512, 16, m))


K, T, S, N, H, W = 512, 2048, 512, 512, 512, 2048


def setup_inputs():
    n = np.random.standard_normal
    s = mx_kscale(K)[:, None]
    u = mx_kscale(H)
    packed_xT = pack_weight(n((K, T)) * s)
    packed_w1 = pack_fp4(n((K, H)) / np.sqrt(K) / s)
    packed_w2 = pack_fp4(n((H, N)) / np.sqrt(2 * H) / u[:, None])
    packed_w3 = pack_fp4(n((K, N)) / np.sqrt(2 * K) / s)
    return {
        "x_words": packed_xT[0],
        "x_scales": packed_xT[1],
        "w1_words": packed_w1[0],
        "w1_scales": packed_w1[1],
        "gn": (np.random.uniform(0.5, 1.5, (H, 1)) * u[:, None]).astype(np.float32),
        "w2_words": packed_w2[0],
        "w2_scales": packed_w2[1],
        "w3_words": packed_w3[0],
        "w3_scales": packed_w3[1],
        "offs": striped(np.random.permutation(T)[:S]),
        "n1": striped8(np.stack([np.random.permutation(S) for _ in range(8)])),
        "n2": striped8(np.stack([np.random.permutation(S) for _ in range(8)])),
        "two": striped(np.random.permutation(T)[:S]),
        "n3": striped(np.random.randint(0, S, W)),
    }


def reference(x_words, x_scales, w1_words, w1_scales, gn, w2_words, w2_scales, w3_words, w3_scales, offs, n1, n2, two, n3):
    xq = unpack_weight(x_words, x_scales)[:, unstriped(offs)]
    y = unpack_fp4(w1_words, w1_scales).T @ xq
    z = f64(gn) * (np.maximum(y * (sigmoid(y[np.arange(H)[:, None], runs(n1, H)])), y[np.arange(H)[:, None], runs(n2, H)]))
    x_two = unpack_weight(x_words, x_scales)[:, unstriped(two)]
    h = unpack_fp4(w2_words, w2_scales).T @ mxq(z, 0, "e4m3") + unpack_fp4(w3_words, w3_scales).T @ x_two
    ex = np.exp(h)
    mb = ex[:, unstriped(n3)]
    ms = mb.reshape(N, S, 4).sum(axis=2)
    out_0 = np.log(ms + ex) - h
    return (out_0,) + planes(out_0)

@@ -1,0 +1,244 @@
+from contextlib import ExitStack
+
+import concourse.mybir as mybir
+
+K, T, S, N, H, W = 512, 2048, 512, 512, 512, 2048
+FLOPS = 2 * S * (K * H + H * N + K * N)
+
+F32 = mybir.dt.float32
+BF16 = mybir.dt.bfloat16
+I32 = mybir.dt.int32
+U32 = mybir.dt.uint32
+U16 = mybir.dt.uint16
+U8 = mybir.dt.uint8
+FP8X4 = mybir.dt.float8_e4m3fn_x4
+FP4X4 = mybir.dt.float4_e2m1fn_x4
+ALU = mybir.AluOpType
+ACT = mybir.ActivationFunctionType
+
+P = 128
+PACK = 4
+QUADS = 4
+GROUP = 16
+MEMBERS = 4
+SPARE = 16
+Z_WIDTHS = (256, 128, 128)
+OUT_WIDTHS = (128, 128, 128, 128)
+VECTOR_TILES = (4, 1, 1, 1)
+
+
+def spans(widths):
+    out, start = [], 0
+    for w in widths:
+        out.append((start, w))
+        start = start + w
+    return out
+
+
+def tile_picked_mixingmaxglse_none_po_kernel(
+    tc, x_words, x_scales, w1_words, w1_scales, gn, w2_words, w2_scales, w3_words, w3_scales,
+    offs, n1, n2, two, n3, out_0, out_1, out_2,
+):
+    nc = tc.nc
+
+    with ExitStack() as ctx:
+        keep = ctx.enter_context(tc.tile_pool(name="keep", bufs=1))
+        psum = ctx.enter_context(tc.psum_pool(name="psum", bufs=1))
+
+        def load_list(src, name):
+            tile = keep.tile(list(src.shape), U16, name=name)
+            nc.sync.dma_start(tile[:], src)
+            return tile
+
+        def load_scale_rows(engines, plane, src):
+            for q in range(QUADS):
+                engines[q].dma_start(plane[32 * q : 32 * q + 4, :].bitcast(I32), src[0, 4 * q : 4 * q + 4, :].bitcast(I32))
+
+        def load_words(src, name):
+            raw = keep.tile([P, 2 * N], U8, name=name)
+            nc.sync.dma_start(raw[:].bitcast(I32), src[0].bitcast(I32))
+            return raw
+
+        def zeroed_plane(width, name):
+            plane = keep.tile([P, width], U8, name=name)
+            nc.gpsimd.memset(plane[:].bitcast(I32), 0)
+            return plane
+
+        def deal(raw_words, raw_scales, name):
+            words = keep.tile([P, 2 * N], U8, name=name + "_words", tag="dealt_words", align_bytes=64)
+            scales = keep.tile([P, N], U8, name=name + "_scales", tag="dealt_scales", align_bytes=64)
+            nc.vector.tensor_copy(
+                out=words[:].rearrange("p (t m b) -> p t m b", t=PACK, b=2),
+                in_=raw_words[:].rearrange("p (m t b) -> p t m b", t=PACK, b=2),
+            )
+            nc.vector.tensor_copy(
+                out=scales[:].rearrange("p (t m) -> p t m", t=PACK),
+                in_=raw_scales[:].rearrange("p (m t) -> p t m", t=PACK),
+            )
+            return words, scales
+
+        def pick(lst, name):
+            words = keep.tile([P, S], U32, name=name + "_words", tag="picked_words", align_bytes=64)
+            scales = keep.tile([P, S], U8, name=name + "_scales", tag="picked_scales", align_bytes=64)
+            nc.vector.tensor_copy(words[:], x_table[:].bitcast(U32).indirect(lst[:]))
+            nc.vector.tensor_copy(scales[:], x_plane[:].indirect(lst[:]))
+            return words, scales
+
+        def product(bank, cols, weights, t, moving, mcols, start, stop):
+            nc.tensor.matmul_mx(
+                out=bank[:, cols],
+                lhsT=weights[0][:, 2 * P * t : 2 * P * (t + 1)].bitcast(FP4X4),
+                lhsT_scale=weights[1][:, P * t : P * (t + 1)],
+                rhs=moving[0][:, mcols].bitcast(FP8X4),
+                rhs_scale=moving[1][:, mcols],
+                start=start,
+                stop=stop,
+            )
+
+        x_plane = zeroed_plane(T, "x_plane")
+        w1_plane = zeroed_plane(H, "w1_plane")
+        offs_t = load_list(offs, "offs_t")
+        w1_raw = load_words(w1_words, "w1_raw")
+        x_table = keep.tile([P, T], I32, name="x_table")
+        nc.sync.dma_start(x_table[:], x_words[0].rearrange("p n t -> p (n t)").bitcast(I32))
+        load_scale_rows([nc.scalar] * QUADS, x_plane, x_scales)
+        load_scale_rows([nc.sync] * (QUADS - 1) + [nc.gpsimd], w1_plane, w1_scales)
+        w3_plane = zeroed_plane(N, "w3_plane")
+        w2_plane = zeroed_plane(N, "w2_plane")
+        two_t = load_list(two, "two_t")
+        n1_t = load_list(n1, "n1_t")
+        n2_t = load_list(n2, "n2_t")
+        w3_raw = load_words(w3_words, "w3_raw")
+        load_scale_rows([nc.sync] * QUADS, w3_plane, w3_scales)
+        w2_raw = load_words(w2_words, "w2_raw")
+        load_scale_rows([nc.sync] * QUADS, w2_plane, w2_scales)
+        gain = keep.tile([P, PACK], F32, name="gain")
+        nc.sync.dma_start(gain[:], gn.rearrange("(p t) o -> p (t o)", t=PACK))
+        n3_t = load_list(n3, "n3_t")
+
+        ex = [keep.tile([P, S + SPARE], F32, name="ex%d" % t) for t in range(PACK)]
+        for t in range(PACK):
+            nc.gpsimd.memset(ex[t][:, S:], 0.0)
+
+        every = slice(0, S)
+        w1 = deal(w1_raw, w1_plane, "w1")
+        x_one = pick(offs_t, "x_one")
+        y_bank = [psum.tile([P, S], F32, name="y_bank%d" % t) for t in range(PACK)]
+        h_bank = [psum.tile([P, S], F32, name="h_bank%d" % t) for t in range(PACK)]
+        y = [keep.tile([P, S], F32, name="y%d" % t) for t in range(PACK)]
+        for t in range(PACK):
+            product(y_bank[t], every, w1, t, x_one, every, True, True)
+        for t in range(PACK):
+            if t < PACK - 1:
+                nc.vector.tensor_copy(y[t][:], y_bank[t][:])
+
+        x_two = pick(two_t, "x_two")
+        w3 = deal(w3_raw, w3_plane, "w3")
+        for t in range(PACK):
+            product(h_bank[t], every, w3, t, x_two, every, True, False)
+        w2 = deal(w2_raw, w2_plane, "w2")
+
+        z_spans = spans(Z_WIDTHS)
+        for c, (c0, cw) in enumerate(z_spans):
+            cols = slice(c0, c0 + cw)
+            entries = slice(c0 // GROUP, (c0 + cw) // GROUP)
+            gate = keep.tile([P, PACK, cw], F32, name="gate%d" % c)
+            other = keep.tile([P, PACK, cw], F32, name="other%d" % c)
+            gated = keep.tile([P, PACK, cw], F32, name="gated%d" % c)
+            larger = keep.tile([P, PACK, cw], F32, name="larger%d" % c)
+            z_bf = keep.tile([P, cw, PACK], BF16, name="z_bf%d" % c, align_bytes=64)
+            z_words = keep.tile([P, cw], U32, name="z_words%d" % c, align_bytes=64)
+            z_scales = keep.tile([P, cw], U8, name="z_scales%d" % c, align_bytes=64)
+            for t in range(PACK):
+                if c == 0 and t == PACK - 1:
+                    nc.scalar.activation(y[t][:], y_bank[t][:], ACT.Copy)
+                nc.scalar.activation(gate[:, t, :], y[t][:].indirect(n1_t[:, entries]), ACT.Sigmoid)
+                nc.scalar.activation(other[:, t, :], y[t][:].indirect(n2_t[:, entries]), ACT.Copy)
+                nc.vector.tensor_tensor(gated[:, t, :], gate[:, t, :], y_bank[t][:, cols], ALU.mult)
+                if t % 2 == 1:
+                    pair = slice(t - 1, t + 1)
+                    nc.vector.tensor_tensor(larger[:, pair, :], gated[:, pair, :], other[:, pair, :], ALU.max)
+            nc.vector.tensor_tensor(
+                z_bf[:].rearrange("p (c i) t -> p c t i", i=2),
+                larger[:].rearrange("p t (c i) -> p c t i", i=2),
+                gain[:].unsqueeze(1).unsqueeze(3).to_broadcast([P, cw // 2, PACK, 2]),
+                ALU.mult,
+            )
+            nc.vector.quantize_mx(
+                out=z_words[:].bitcast(FP8X4), scales=z_scales[:], in_=z_bf[:].rearrange("p c t -> p (c t)")
+            )
+            for t in range(PACK):
+                product(h_bank[t], cols, w2, t, (z_words, z_scales), slice(0, cw), False, c == len(z_spans) - 1)
+
+        inverse = keep.tile([P, PACK, S], F32, name="inverse")
+        for t in range(PACK):
+            nc.scalar.activation(ex[t][:, :S], h_bank[t][:], ACT.Exp)
+        for t in range(PACK):
+            nc.scalar.activation(inverse[:, t, :], h_bank[t][:], ACT.Exp, scale=-1.0)
+
+        out_rows = out_0.rearrange("(p t) j -> p t j", t=PACK)
+        out_words = out_1[0].rearrange("p n t -> p (n t)").bitcast(I32)
+        o_words = keep.tile([P, S], U32, name="o_words", align_bytes=64)
+        o_scales = keep.tile([P, S], U8, name="o_scales", align_bytes=64)
+        o_spans = spans(OUT_WIDTHS)
+        members, ratio, result = {}, {}, {}
+
+        def fetch(c):
+            c0, cw = o_spans[c]
+            entries = slice(MEMBERS * c0 // GROUP, MEMBERS * (c0 + cw) // GROUP)
+            members[c] = [keep.tile([P, 2, MEMBERS * cw], F32, name="members%d_%d" % (c, u)) for u in range(2)]
+            for t in range(PACK):
+                dst = members[c][t // 2][:, t % 2, :]
+                src = ex[t][:].indirect(n3_t[:, entries])
+                if t >= PACK - VECTOR_TILES[c]:
+                    nc.vector.tensor_copy(dst, src)
+                else:
+                    nc.scalar.activation(dst, src, ACT.Copy)
+
+        def add_up(c):
+            c0, cw = o_spans[c]
+            pairs = keep.tile([P, PACK, cw, 2], F32, name="pairs%d" % c)
+            sums = keep.tile([P, PACK, cw], F32, name="sums%d" % c)
+            ratio[c] = keep.tile([P, PACK, cw], F32, name="ratio%d" % c)
+            for u in range(2):
+                four = members[c][u][:].rearrange("p t (j m) -> p (t j) m", m=MEMBERS)
+                nc.vector.tensor_tensor(
+                    pairs[:, 2 * u : 2 * u + 2, :, :].rearrange("p t j e -> p (t j) e"), four[:, :, 0:2], four[:, :, 2:4], ALU.add
+                )
+            nc.vector.tensor_tensor(sums[:], pairs[:, :, :, 0], pairs[:, :, :, 1], ALU.add)
+            nc.vector.tensor_tensor(ratio[c][:], sums[:], inverse[:, :, c0 : c0 + cw], ALU.mult)
+
+        def take_log(c):
+            c0, cw = o_spans[c]
+            result[c] = keep.tile([P, PACK, cw], F32, name="result%d" % c)
+            nc.scalar.activation(result[c][:], ratio[c][:], ACT.Ln, bias=1.0)
+            nc.sync.dma_start(out_rows[:, :, c0 : c0 + cw], result[c][:])
+
+        def hand_on(c):
+            c0, cw = o_spans[c]
+            o_bf = keep.tile([P, cw, PACK], BF16, name="o_bf%d" % c, align_bytes=64)
+            nc.vector.tensor_copy(
+                out=o_bf[:].rearrange("p (c i) t -> p c t i", i=4),
+                in_=result[c][:].rearrange("p t (c i) -> p c t i", i=4),
+            )
+            nc.vector.quantize_mx(
+                out=o_words[:, c0 : c0 + cw].bitcast(FP8X4),
+                scales=o_scales[:, c0 : c0 + cw],
+                in_=o_bf[:].rearrange("p c t -> p (c t)"),
+            )
+
+        n_out = len(o_spans)
+        for c in range(n_out):
+            fetch(c)
+            add_up(c)
+        for c in range(n_out):
+            take_log(c)
+            hand_on(c)
+            if c % 2 == 1:
+                half = slice(o_spans[c - 1][0], o_spans[c][0] + o_spans[c][1])
+                nc.sync.dma_start(out_words[:, half], o_words[:, half].bitcast(I32))
+        for q in range(QUADS):
+            engine = nc.scalar if q % 2 else nc.sync
+            engine.dma_start(
+                out_2[0, 4 * q : 4 * q + 4, :].bitcast(I32), o_scales[32 * q : 32 * q + 4, :].bitcast(I32)
+            )

@@ -22,8 +22,11 @@ QUADS = 4
 GROUP = 16
 MEMBERS = 4
 SPARE = 16
-Z_WIDTHS = (256, 128, 128)
+Z_WIDTHS = (128, 256, 128)
 OUT_WIDTHS = (128, 128, 128, 128)
+VECTOR_EMPTIES = (1,)
+VECTOR_OTHER = (0, 2, 0)
+SCALAR_ROUNDS = ()
 VECTOR_TILES = (4, 1, 1, 1)
 
 
@@ -54,19 +57,19 @@ def tile_picked_mixingmaxglse_none_po_kernel(
             for q in range(QUADS):
                 engines[q].dma_start(plane[32 * q : 32 * q + 4, :].bitcast(I32), src[0, 4 * q : 4 * q + 4, :].bitcast(I32))
 
-        def load_words(src, name):
-            raw = keep.tile([P, 2 * N], U8, name=name)
-            nc.sync.dma_start(raw[:].bitcast(I32), src[0].bitcast(I32))
+        def load_words(engine, src, name, slot):
+            raw = keep.tile([P, 2 * N], U8, name=name, tag=slot)
+            engine.dma_start(raw[:].bitcast(I32), src[0].bitcast(I32))
             return raw
 
-        def zeroed_plane(width, name):
+        def zeroed_plane(engine, width, name):
             plane = keep.tile([P, width], U8, name=name)
-            nc.gpsimd.memset(plane[:].bitcast(I32), 0)
+            engine.memset(plane[:].bitcast(I32), 0)
             return plane
 
-        def deal(raw_words, raw_scales, name):
-            words = keep.tile([P, 2 * N], U8, name=name + "_words", tag="dealt_words", align_bytes=64)
-            scales = keep.tile([P, N], U8, name=name + "_scales", tag="dealt_scales", align_bytes=64)
+        def deal(raw_words, raw_scales, name, slot):
+            words = keep.tile([P, 2 * N], U8, name=name + "_words", tag=slot + "_words", align_bytes=64)
+            scales = keep.tile([P, N], U8, name=name + "_scales", tag=slot + "_scales", align_bytes=64)
             nc.vector.tensor_copy(
                 out=words[:].rearrange("p (t m b) -> p t m b", t=PACK, b=2),
                 in_=raw_words[:].rearrange("p (m t b) -> p t m b", t=PACK, b=2),
@@ -77,11 +80,13 @@ def tile_picked_mixingmaxglse_none_po_kernel(
             )
             return words, scales
 
-        def pick(lst, name):
-            words = keep.tile([P, S], U32, name=name + "_words", tag="picked_words", align_bytes=64)
-            scales = keep.tile([P, S], U8, name=name + "_scales", tag="picked_scales", align_bytes=64)
-            nc.vector.tensor_copy(words[:], x_table[:].bitcast(U32).indirect(lst[:]))
+        def pick(lst, name, parts):
+            words = keep.tile([P, S], U32, name=name + "_words", align_bytes=64)
+            scales = keep.tile([P, S], U8, name=name + "_scales", align_bytes=64)
             nc.vector.tensor_copy(scales[:], x_plane[:].indirect(lst[:]))
+            for part in parts:
+                entries = slice(part.start // GROUP, part.stop // GROUP)
+                nc.vector.tensor_copy(words[:, part], x_table[:].bitcast(U32).indirect(lst[:, entries]))
             return words, scales
 
         def product(bank, cols, weights, t, moving, mcols, start, stop):
@@ -95,69 +100,88 @@ def tile_picked_mixingmaxglse_none_po_kernel(
                 stop=stop,
             )
 
-        x_plane = zeroed_plane(T, "x_plane")
-        w1_plane = zeroed_plane(H, "w1_plane")
+        w_plane = zeroed_plane(nc.gpsimd, H, "w_plane")
+        x_plane = zeroed_plane(nc.vector, T, "x_plane")
+        x_rows = keep.tile([P, T], U8, name="x_rows")
+        load_scale_rows([nc.sync, nc.scalar] * 2, x_rows, x_scales)
         offs_t = load_list(offs, "offs_t")
-        w1_raw = load_words(w1_words, "w1_raw")
+        w1_raw = load_words(nc.scalar, w1_words, "w1_raw", "raw_first")
         x_table = keep.tile([P, T], I32, name="x_table")
         nc.sync.dma_start(x_table[:], x_words[0].rearrange("p n t -> p (n t)").bitcast(I32))
-        load_scale_rows([nc.scalar] * QUADS, x_plane, x_scales)
-        load_scale_rows([nc.sync] * (QUADS - 1) + [nc.gpsimd], w1_plane, w1_scales)
-        w3_plane = zeroed_plane(N, "w3_plane")
-        w2_plane = zeroed_plane(N, "w2_plane")
+        load_scale_rows([nc.scalar, nc.sync, nc.scalar, nc.gpsimd], w_plane, w1_scales)
         two_t = load_list(two, "two_t")
         n1_t = load_list(n1, "n1_t")
         n2_t = load_list(n2, "n2_t")
-        w3_raw = load_words(w3_words, "w3_raw")
+        w3_plane = zeroed_plane(nc.vector, N, "w3_plane")
+        w3_raw = load_words(nc.sync, w3_words, "w3_raw", "raw_second")
         load_scale_rows([nc.sync] * QUADS, w3_plane, w3_scales)
-        w2_raw = load_words(w2_words, "w2_raw")
-        load_scale_rows([nc.sync] * QUADS, w2_plane, w2_scales)
+        n3_t = load_list(n3, "n3_t")
         gain = keep.tile([P, PACK], F32, name="gain")
         nc.sync.dma_start(gain[:], gn.rearrange("(p t) o -> p (t o)", t=PACK))
-        n3_t = load_list(n3, "n3_t")
+        warm_in = keep.tile([P, 1], F32, name="warm_in")
+        warm_out = keep.tile([P, 1], F32, name="warm_out")
+        nc.gpsimd.memset(warm_in[:], 0.0)
+        nc.scalar.activation(warm_out[:], warm_in[:], ACT.Sigmoid)
+        for q in range(QUADS):
+            rows = slice(32 * q, 32 * q + 4)
+            nc.vector.tensor_copy(x_plane[rows, :].bitcast(I32), x_rows[rows, :].bitcast(I32))
 
         ex = [keep.tile([P, S + SPARE], F32, name="ex%d" % t) for t in range(PACK)]
         for t in range(PACK):
-            nc.gpsimd.memset(ex[t][:, S:], 0.0)
+            nc.vector.memset(ex[t][:, S:], 0.0)
 
         every = slice(0, S)
-        w1 = deal(w1_raw, w1_plane, "w1")
-        x_one = pick(offs_t, "x_one")
-        y_bank = [psum.tile([P, S], F32, name="y_bank%d" % t) for t in range(PACK)]
+        halves = [slice(0, S // 2), slice(S // 2, S)]
+        z_spans = spans(Z_WIDTHS)
+        early = [slice(c0, c0 + cw) for c0, cw in z_spans[:-1]]
+        split, late_width = z_spans[-1]
+        w1 = deal(w1_raw, w_plane, "w1", "token_side")
+        w2_raw = load_words(nc.sync, w2_words, "w2_raw", "raw_first")
+        load_scale_rows([nc.sync] * QUADS, w_plane, w2_scales)
+        x_one = pick(offs_t, "x_one", halves)
+        y_bank = [psum.tile([P, S], F32, name="y_bank%d" % t, tag="bank%d" % t) for t in range(PACK)]
         h_bank = [psum.tile([P, S], F32, name="h_bank%d" % t) for t in range(PACK)]
         y = [keep.tile([P, S], F32, name="y%d" % t) for t in range(PACK)]
         for t in range(PACK):
-            product(y_bank[t], every, w1, t, x_one, every, True, True)
-        for t in range(PACK):
-            if t < PACK - 1:
-                nc.vector.tensor_copy(y[t][:], y_bank[t][:])
+            for half in halves:
+                product(y_bank[t], half, w1, t, x_one, half, True, True)
+        nc.scalar.activation(y[0][:], y_bank[0][:], ACT.Copy)
+        for t in VECTOR_EMPTIES:
+            nc.vector.tensor_copy(y[t][:], y_bank[t][:])
 
-        x_two = pick(two_t, "x_two")
-        w3 = deal(w3_raw, w3_plane, "w3")
+        x_two = pick(two_t, "x_two", [every])
+        w3 = deal(w3_raw, w3_plane, "w3", "token_side")
         for t in range(PACK):
-            product(h_bank[t], every, w3, t, x_two, every, True, False)
-        w2 = deal(w2_raw, w2_plane, "w2")
+            for e, part in enumerate(early):
+                product(h_bank[t], part, w3, t, x_two, part, e == 0, False)
+        w2 = deal(w2_raw, w_plane, "w2", "hidden_side")
 
-        z_spans = spans(Z_WIDTHS)
         for c, (c0, cw) in enumerate(z_spans):
             cols = slice(c0, c0 + cw)
             entries = slice(c0 // GROUP, (c0 + cw) // GROUP)
             gate = keep.tile([P, PACK, cw], F32, name="gate%d" % c)
             other = keep.tile([P, PACK, cw], F32, name="other%d" % c)
             gated = keep.tile([P, PACK, cw], F32, name="gated%d" % c)
-            larger = keep.tile([P, PACK, cw], F32, name="larger%d" % c)
+            larger = keep.tile([P, PACK, cw], F32, name="larger%d" % c, tag="larger_last" if c0 == split else "larger%d" % c)
             z_bf = keep.tile([P, cw, PACK], BF16, name="z_bf%d" % c, align_bytes=64)
             z_words = keep.tile([P, cw], U32, name="z_words%d" % c, align_bytes=64)
             z_scales = keep.tile([P, cw], U8, name="z_scales%d" % c, align_bytes=64)
             for t in range(PACK):
-                if c == 0 and t == PACK - 1:
-                    nc.scalar.activation(y[t][:], y_bank[t][:], ACT.Copy)
+                if c == 0 and t + 1 < PACK and t + 1 not in VECTOR_EMPTIES:
+                    nc.scalar.activation(y[t + 1][:], y_bank[t + 1][:], ACT.Copy)
                 nc.scalar.activation(gate[:, t, :], y[t][:].indirect(n1_t[:, entries]), ACT.Sigmoid)
-                nc.scalar.activation(other[:, t, :], y[t][:].indirect(n2_t[:, entries]), ACT.Copy)
+                if t < VECTOR_OTHER[c]:
+                    nc.vector.tensor_copy(other[:, t, :], y[t][:].indirect(n2_t[:, entries]))
+                else:
+                    nc.scalar.activation(other[:, t, :], y[t][:].indirect(n2_t[:, entries]), ACT.Copy)
                 nc.vector.tensor_tensor(gated[:, t, :], gate[:, t, :], y_bank[t][:, cols], ALU.mult)
                 if t % 2 == 1:
                     pair = slice(t - 1, t + 1)
                     nc.vector.tensor_tensor(larger[:, pair, :], gated[:, pair, :], other[:, pair, :], ALU.max)
+            if c0 == split:
+                late_bank = [psum.tile([P, S], F32, name="late_bank%d" % t, tag="bank%d" % t) for t in range(PACK)]
+                for t in range(PACK):
+                    product(late_bank[t], slice(0, cw), w3, t, x_two, cols, True, False)
             nc.vector.tensor_tensor(
                 z_bf[:].rearrange("p (c i) t -> p c t i", i=2),
                 larger[:].rearrange("p t (c i) -> p c t i", i=2),
@@ -168,13 +192,18 @@ def tile_picked_mixingmaxglse_none_po_kernel(
                 out=z_words[:].bitcast(FP8X4), scales=z_scales[:], in_=z_bf[:].rearrange("p c t -> p (c t)")
             )
             for t in range(PACK):
-                product(h_bank[t], cols, w2, t, (z_words, z_scales), slice(0, cw), False, c == len(z_spans) - 1)
+                if c0 == split:
+                    product(late_bank[t], slice(0, cw), w2, t, (z_words, z_scales), slice(0, cw), False, True)
+                else:
+                    product(h_bank[t], cols, w2, t, (z_words, z_scales), slice(0, cw), False, c0 + cw == split)
 
-        inverse = keep.tile([P, PACK, S], F32, name="inverse")
+        inverse = keep.tile([P, PACK, S], F32, name="inverse", tag="larger_last")
         for t in range(PACK):
-            nc.scalar.activation(ex[t][:, :S], h_bank[t][:], ACT.Exp)
+            nc.scalar.activation(ex[t][:, :split], h_bank[t][:, :split], ACT.Exp)
+            nc.scalar.activation(ex[t][:, split:S], late_bank[t][:, :late_width], ACT.Exp)
         for t in range(PACK):
-            nc.scalar.activation(inverse[:, t, :], h_bank[t][:], ACT.Exp, scale=-1.0)
+            nc.scalar.activation(inverse[:, t, :split], h_bank[t][:, :split], ACT.Exp, scale=-1.0)
+            nc.scalar.activation(inverse[:, t, split:], late_bank[t][:, :late_width], ACT.Exp, scale=-1.0)
 
         out_rows = out_0.rearrange("(p t) j -> p t j", t=PACK)
         out_words = out_1[0].rearrange("p n t -> p (n t)").bitcast(I32)
@@ -217,10 +246,12 @@ def tile_picked_mixingmaxglse_none_po_kernel(
         def hand_on(c):
             c0, cw = o_spans[c]
             o_bf = keep.tile([P, cw, PACK], BF16, name="o_bf%d" % c, align_bytes=64)
-            nc.vector.tensor_copy(
-                out=o_bf[:].rearrange("p (c i) t -> p c t i", i=4),
-                in_=result[c][:].rearrange("p t (c i) -> p c t i", i=4),
-            )
+            woven = o_bf[:].rearrange("p (c i) t -> p c t i", i=4)
+            planes = result[c][:].rearrange("p t (c i) -> p c t i", i=4)
+            if c in SCALAR_ROUNDS:
+                nc.scalar.activation(woven, planes, ACT.Copy)
+            else:
+                nc.vector.tensor_copy(out=woven, in_=planes)
             nc.vector.quantize_mx(
                 out=o_words[:, c0 : c0 + cw].bitcast(FP8X4),
                 scales=o_scales[:, c0 : c0 + cw],
@@ -234,9 +265,9 @@ def tile_picked_mixingmaxglse_none_po_kernel(
         for c in range(n_out):
             take_log(c)
             hand_on(c)
-            if c % 2 == 1:
-                half = slice(o_spans[c - 1][0], o_spans[c][0] + o_spans[c][1])
-                nc.sync.dma_start(out_words[:, half], o_words[:, half].bitcast(I32))
+            if c >= n_out - 2:
+                part = slice(0 if c == n_out - 2 else o_spans[c][0], o_spans[c][0] + o_spans[c][1])
+                nc.sync.dma_start(out_words[:, part], o_words[:, part].bitcast(I32))
         for q in range(QUADS):
             engine = nc.scalar if q % 2 else nc.sync
             engine.dma_start(

@@ -22,10 +22,10 @@ QUADS = 4
 GROUP = 16
 MEMBERS = 4
 SPARE = 16
-Z_WIDTHS = (128, 256, 128)
+Z_WIDTHS = (256, 128, 128)
 OUT_WIDTHS = (128, 128, 128, 128)
-VECTOR_EMPTIES = (1,)
-VECTOR_OTHER = (0, 2, 0)
+VECTOR_EMPTIES = (3,)
+VECTOR_OTHER = (2, 0, 0)
 SCALAR_ROUNDS = ()
 VECTOR_TILES = (4, 1, 1, 1)
 
@@ -71,8 +71,8 @@ def tile_picked_mixingmaxglse_none_po_kernel(
             words = keep.tile([P, 2 * N], U8, name=name + "_words", tag=slot + "_words", align_bytes=64)
             scales = keep.tile([P, N], U8, name=name + "_scales", tag=slot + "_scales", align_bytes=64)
             nc.vector.tensor_copy(
-                out=words[:].rearrange("p (t m b) -> p t m b", t=PACK, b=2),
-                in_=raw_words[:].rearrange("p (m t b) -> p t m b", t=PACK, b=2),
+                out=words[:].bitcast(U16).rearrange("p (t m) -> p t m", t=PACK),
+                in_=raw_words[:].bitcast(U16).rearrange("p (m t) -> p t m", t=PACK),
             )
             nc.vector.tensor_copy(
                 out=scales[:].rearrange("p (t m) -> p t m", t=PACK),
@@ -108,7 +108,11 @@ def tile_picked_mixingmaxglse_none_po_kernel(
         w1_raw = load_words(nc.scalar, w1_words, "w1_raw", "raw_first")
         x_table = keep.tile([P, T], I32, name="x_table")
         nc.sync.dma_start(x_table[:], x_words[0].rearrange("p n t -> p (n t)").bitcast(I32))
-        load_scale_rows([nc.scalar, nc.sync, nc.scalar, nc.gpsimd], w_plane, w1_scales)
+        load_scale_rows([nc.scalar, nc.sync] * 2, w_plane, w1_scales)
+        gain = keep.tile([P, PACK], F32, name="gain")
+        nc.scalar.dma_start(gain[:], gn.rearrange("(p t) o -> p (t o)", t=PACK))
+        warm = keep.tile([P, 1], F32, name="warm")
+        nc.scalar.activation(warm[:], gain[:, 0:1], ACT.Sigmoid)
         two_t = load_list(two, "two_t")
         n1_t = load_list(n1, "n1_t")
         n2_t = load_list(n2, "n2_t")
@@ -116,12 +120,6 @@ def tile_picked_mixingmaxglse_none_po_kernel(
         w3_raw = load_words(nc.sync, w3_words, "w3_raw", "raw_second")
         load_scale_rows([nc.sync] * QUADS, w3_plane, w3_scales)
         n3_t = load_list(n3, "n3_t")
-        gain = keep.tile([P, PACK], F32, name="gain")
-        nc.sync.dma_start(gain[:], gn.rearrange("(p t) o -> p (t o)", t=PACK))
-        warm_in = keep.tile([P, 1], F32, name="warm_in")
-        warm_out = keep.tile([P, 1], F32, name="warm_out")
-        nc.gpsimd.memset(warm_in[:], 0.0)
-        nc.scalar.activation(warm_out[:], warm_in[:], ACT.Sigmoid)
         for q in range(QUADS):
             rows = slice(32 * q, 32 * q + 4)
             nc.vector.tensor_copy(x_plane[rows, :].bitcast(I32), x_rows[rows, :].bitcast(I32))

@@ -2,7 +2,7 @@ from contextlib import ExitStack
 
 import concourse.mybir as mybir
 
-K, T, S, N, H, W = 512, 2048, 512, 512, 512, 2048
+K, T, S, N, H = 512, 2048, 512, 512, 512
 FLOPS = 2 * S * (K * H + H * N + K * N)
 
 F32 = mybir.dt.float32
@@ -23,19 +23,12 @@ GROUP = 16
 MEMBERS = 4
 SPARE = 16
 Z_WIDTHS = (256, 128, 128)
-OUT_WIDTHS = (128, 128, 128, 128)
-VECTOR_EMPTIES = (3,)
-VECTOR_OTHER = (2, 0, 0)
-SCALAR_ROUNDS = ()
-VECTOR_TILES = (4, 1, 1, 1)
+VECTOR_N2_TILES = 3
+OUT_WIDTH = 128
 
 
-def spans(widths):
-    out, start = [], 0
-    for w in widths:
-        out.append((start, w))
-        start = start + w
-    return out
+def entries_of(first, last):
+    return slice(first // GROUP, last // GROUP)
 
 
 def tile_picked_mixingmaxglse_none_po_kernel(
@@ -53,13 +46,13 @@ def tile_picked_mixingmaxglse_none_po_kernel(
             nc.sync.dma_start(tile[:], src)
             return tile
 
-        def load_scale_rows(engines, plane, src):
+        def load_scale_rows(queues, plane, src):
             for q in range(QUADS):
-                engines[q].dma_start(plane[32 * q : 32 * q + 4, :].bitcast(I32), src[0, 4 * q : 4 * q + 4, :].bitcast(I32))
+                queues[q].dma_start(plane[32 * q : 32 * q + 4, :].bitcast(I32), src[0, 4 * q : 4 * q + 4, :].bitcast(I32))
 
-        def load_words(engine, src, name, slot):
+        def load_words(queue, src, name, slot):
             raw = keep.tile([P, 2 * N], U8, name=name, tag=slot)
-            engine.dma_start(raw[:].bitcast(I32), src[0].bitcast(I32))
+            queue.dma_start(raw[:].bitcast(I32), src[0].bitcast(I32))
             return raw
 
         def zeroed_plane(engine, width, name):
@@ -74,7 +67,7 @@ def tile_picked_mixingmaxglse_none_po_kernel(
                 out=words[:].bitcast(U16).rearrange("p (t m) -> p t m", t=PACK),
                 in_=raw_words[:].bitcast(U16).rearrange("p (m t) -> p t m", t=PACK),
             )
-            nc.vector.tensor_copy(
+            nc.gpsimd.tensor_copy(
                 out=scales[:].rearrange("p (t m) -> p t m", t=PACK),
                 in_=raw_scales[:].rearrange("p (m t) -> p t m", t=PACK),
             )
@@ -85,17 +78,17 @@ def tile_picked_mixingmaxglse_none_po_kernel(
             scales = keep.tile([P, S], U8, name=name + "_scales", align_bytes=64)
             nc.vector.tensor_copy(scales[:], x_plane[:].indirect(lst[:]))
             for part in parts:
-                entries = slice(part.start // GROUP, part.stop // GROUP)
-                nc.vector.tensor_copy(words[:, part], x_table[:].bitcast(U32).indirect(lst[:, entries]))
+                picked = x_table[:].bitcast(U32).indirect(lst[:, entries_of(part.start, part.stop)])
+                nc.vector.tensor_copy(words[:, part], picked)
             return words, scales
 
-        def product(bank, cols, weights, t, moving, mcols, start, stop):
+        def product(bank, bank_cols, weights, t, moving, moving_cols, start, stop):
             nc.tensor.matmul_mx(
-                out=bank[:, cols],
+                out=bank[:, bank_cols],
                 lhsT=weights[0][:, 2 * P * t : 2 * P * (t + 1)].bitcast(FP4X4),
                 lhsT_scale=weights[1][:, P * t : P * (t + 1)],
-                rhs=moving[0][:, mcols].bitcast(FP8X4),
-                rhs_scale=moving[1][:, mcols],
+                rhs=moving[0][:, moving_cols].bitcast(FP8X4),
+                rhs_scale=moving[1][:, moving_cols],
                 start=start,
                 stop=stop,
             )
@@ -130,9 +123,9 @@ def tile_picked_mixingmaxglse_none_po_kernel(
 
         every = slice(0, S)
         halves = [slice(0, S // 2), slice(S // 2, S)]
-        z_spans = spans(Z_WIDTHS)
-        early = [slice(c0, c0 + cw) for c0, cw in z_spans[:-1]]
-        split, late_width = z_spans[-1]
+        z_starts = [sum(Z_WIDTHS[:c]) for c in range(len(Z_WIDTHS))]
+        stretches = [slice(c0, c0 + cw) for c0, cw in zip(z_starts, Z_WIDTHS)]
+        split, late_width = z_starts[-1], Z_WIDTHS[-1]
         w1 = deal(w1_raw, w_plane, "w1", "token_side")
         w2_raw = load_words(nc.sync, w2_words, "w2_raw", "raw_first")
         load_scale_rows([nc.sync] * QUADS, w_plane, w2_scales)
@@ -144,31 +137,30 @@ def tile_picked_mixingmaxglse_none_po_kernel(
             for half in halves:
                 product(y_bank[t], half, w1, t, x_one, half, True, True)
         nc.scalar.activation(y[0][:], y_bank[0][:], ACT.Copy)
-        for t in VECTOR_EMPTIES:
-            nc.vector.tensor_copy(y[t][:], y_bank[t][:])
 
         x_two = pick(two_t, "x_two", [every])
         w3 = deal(w3_raw, w3_plane, "w3", "token_side")
         for t in range(PACK):
-            for e, part in enumerate(early):
-                product(h_bank[t], part, w3, t, x_two, part, e == 0, False)
+            for c, cols in enumerate(stretches[:-1]):
+                product(h_bank[t], cols, w3, t, x_two, cols, c == 0, False)
         w2 = deal(w2_raw, w_plane, "w2", "hidden_side")
 
-        for c, (c0, cw) in enumerate(z_spans):
-            cols = slice(c0, c0 + cw)
-            entries = slice(c0 // GROUP, (c0 + cw) // GROUP)
+        for c, cols in enumerate(stretches):
+            cw = Z_WIDTHS[c]
+            late = cols.start == split
+            entries = entries_of(cols.start, cols.stop)
             gate = keep.tile([P, PACK, cw], F32, name="gate%d" % c)
             other = keep.tile([P, PACK, cw], F32, name="other%d" % c)
             gated = keep.tile([P, PACK, cw], F32, name="gated%d" % c)
-            larger = keep.tile([P, PACK, cw], F32, name="larger%d" % c, tag="larger_last" if c0 == split else "larger%d" % c)
+            larger = keep.tile([P, PACK, cw], F32, name="larger%d" % c, tag="larger_last" if late else "larger%d" % c)
             z_bf = keep.tile([P, cw, PACK], BF16, name="z_bf%d" % c, align_bytes=64)
             z_words = keep.tile([P, cw], U32, name="z_words%d" % c, align_bytes=64)
             z_scales = keep.tile([P, cw], U8, name="z_scales%d" % c, align_bytes=64)
             for t in range(PACK):
-                if c == 0 and t + 1 < PACK and t + 1 not in VECTOR_EMPTIES:
+                if c == 0 and t + 1 < PACK:
                     nc.scalar.activation(y[t + 1][:], y_bank[t + 1][:], ACT.Copy)
                 nc.scalar.activation(gate[:, t, :], y[t][:].indirect(n1_t[:, entries]), ACT.Sigmoid)
-                if t < VECTOR_OTHER[c]:
+                if c == 0 and t < VECTOR_N2_TILES:
                     nc.vector.tensor_copy(other[:, t, :], y[t][:].indirect(n2_t[:, entries]))
                 else:
                     nc.scalar.activation(other[:, t, :], y[t][:].indirect(n2_t[:, entries]), ACT.Copy)
@@ -176,7 +168,7 @@ def tile_picked_mixingmaxglse_none_po_kernel(
                 if t % 2 == 1:
                     pair = slice(t - 1, t + 1)
                     nc.vector.tensor_tensor(larger[:, pair, :], gated[:, pair, :], other[:, pair, :], ALU.max)
-            if c0 == split:
+            if late:
                 late_bank = [psum.tile([P, S], F32, name="late_bank%d" % t, tag="bank%d" % t) for t in range(PACK)]
                 for t in range(PACK):
                     product(late_bank[t], slice(0, cw), w3, t, x_two, cols, True, False)
@@ -190,10 +182,10 @@ def tile_picked_mixingmaxglse_none_po_kernel(
                 out=z_words[:].bitcast(FP8X4), scales=z_scales[:], in_=z_bf[:].rearrange("p c t -> p (c t)")
             )
             for t in range(PACK):
-                if c0 == split:
+                if late:
                     product(late_bank[t], slice(0, cw), w2, t, (z_words, z_scales), slice(0, cw), False, True)
                 else:
-                    product(h_bank[t], cols, w2, t, (z_words, z_scales), slice(0, cw), False, c0 + cw == split)
+                    product(h_bank[t], cols, w2, t, (z_words, z_scales), slice(0, cw), False, cols.stop == split)
 
         inverse = keep.tile([P, PACK, S], F32, name="inverse", tag="larger_last")
         for t in range(PACK):
@@ -203,71 +195,50 @@ def tile_picked_mixingmaxglse_none_po_kernel(
             nc.scalar.activation(inverse[:, t, :split], h_bank[t][:, :split], ACT.Exp, scale=-1.0)
             nc.scalar.activation(inverse[:, t, split:], late_bank[t][:, :late_width], ACT.Exp, scale=-1.0)
 
-        out_rows = out_0.rearrange("(p t) j -> p t j", t=PACK)
-        out_words = out_1[0].rearrange("p n t -> p (n t)").bitcast(I32)
+        n_out = S // OUT_WIDTH
+        out_cols = [slice(c * OUT_WIDTH, (c + 1) * OUT_WIDTH) for c in range(n_out)]
         o_words = keep.tile([P, S], U32, name="o_words", align_bytes=64)
         o_scales = keep.tile([P, S], U8, name="o_scales", align_bytes=64)
-        o_spans = spans(OUT_WIDTHS)
-        members, ratio, result = {}, {}, {}
-
-        def fetch(c):
-            c0, cw = o_spans[c]
-            entries = slice(MEMBERS * c0 // GROUP, MEMBERS * (c0 + cw) // GROUP)
-            members[c] = [keep.tile([P, 2, MEMBERS * cw], F32, name="members%d_%d" % (c, u)) for u in range(2)]
+        ratio = []
+        for c, cols in enumerate(out_cols):
+            entries = entries_of(MEMBERS * cols.start, MEMBERS * cols.stop)
+            members = [keep.tile([P, 2, MEMBERS * OUT_WIDTH], F32, name="members%d_%d" % (c, u)) for u in range(2)]
             for t in range(PACK):
-                dst = members[c][t // 2][:, t % 2, :]
-                src = ex[t][:].indirect(n3_t[:, entries])
-                if t >= PACK - VECTOR_TILES[c]:
-                    nc.vector.tensor_copy(dst, src)
+                fetched = ex[t][:].indirect(n3_t[:, entries])
+                if c == 0 or t == PACK - 1:
+                    nc.vector.tensor_copy(members[t // 2][:, t % 2, :], fetched)
                 else:
-                    nc.scalar.activation(dst, src, ACT.Copy)
-
-        def add_up(c):
-            c0, cw = o_spans[c]
-            pairs = keep.tile([P, PACK, cw, 2], F32, name="pairs%d" % c)
-            sums = keep.tile([P, PACK, cw], F32, name="sums%d" % c)
-            ratio[c] = keep.tile([P, PACK, cw], F32, name="ratio%d" % c)
+                    nc.scalar.activation(members[t // 2][:, t % 2, :], fetched, ACT.Copy)
+            pairs = keep.tile([P, PACK, OUT_WIDTH, 2], F32, name="pairs%d" % c)
+            sums = keep.tile([P, PACK, OUT_WIDTH], F32, name="sums%d" % c)
+            ratio.append(keep.tile([P, PACK, OUT_WIDTH], F32, name="ratio%d" % c))
             for u in range(2):
-                four = members[c][u][:].rearrange("p t (j m) -> p (t j) m", m=MEMBERS)
+                four = members[u][:].rearrange("p t (j m) -> p (t j) m", m=MEMBERS)
                 nc.vector.tensor_tensor(
                     pairs[:, 2 * u : 2 * u + 2, :, :].rearrange("p t j e -> p (t j) e"), four[:, :, 0:2], four[:, :, 2:4], ALU.add
                 )
             nc.vector.tensor_tensor(sums[:], pairs[:, :, :, 0], pairs[:, :, :, 1], ALU.add)
-            nc.vector.tensor_tensor(ratio[c][:], sums[:], inverse[:, :, c0 : c0 + cw], ALU.mult)
+            nc.vector.tensor_tensor(ratio[c][:], sums[:], inverse[:, :, cols], ALU.mult)
 
-        def take_log(c):
-            c0, cw = o_spans[c]
-            result[c] = keep.tile([P, PACK, cw], F32, name="result%d" % c)
-            nc.scalar.activation(result[c][:], ratio[c][:], ACT.Ln, bias=1.0)
-            nc.sync.dma_start(out_rows[:, :, c0 : c0 + cw], result[c][:])
-
-        def hand_on(c):
-            c0, cw = o_spans[c]
-            o_bf = keep.tile([P, cw, PACK], BF16, name="o_bf%d" % c, align_bytes=64)
-            woven = o_bf[:].rearrange("p (c i) t -> p c t i", i=4)
-            planes = result[c][:].rearrange("p t (c i) -> p c t i", i=4)
-            if c in SCALAR_ROUNDS:
-                nc.scalar.activation(woven, planes, ACT.Copy)
-            else:
-                nc.vector.tensor_copy(out=woven, in_=planes)
+        out_rows = out_0.rearrange("(p t) j -> p t j", t=PACK)
+        out_words = out_1[0].rearrange("p n t -> p (n t)").bitcast(I32)
+        for c, cols in enumerate(out_cols):
+            result = keep.tile([P, PACK, OUT_WIDTH], F32, name="result%d" % c)
+            nc.scalar.activation(result[:], ratio[c][:], ACT.Ln, bias=1.0)
+            nc.sync.dma_start(out_rows[:, :, cols], result[:])
+            o_bf = keep.tile([P, OUT_WIDTH, PACK], BF16, name="o_bf%d" % c, align_bytes=64)
+            nc.vector.tensor_copy(
+                out=o_bf[:].rearrange("p (c i) t -> p c t i", i=4),
+                in_=result[:].rearrange("p t (c i) -> p c t i", i=4),
+            )
             nc.vector.quantize_mx(
-                out=o_words[:, c0 : c0 + cw].bitcast(FP8X4),
-                scales=o_scales[:, c0 : c0 + cw],
+                out=o_words[:, cols].bitcast(FP8X4),
+                scales=o_scales[:, cols],
                 in_=o_bf[:].rearrange("p c t -> p (c t)"),
             )
-
-        n_out = len(o_spans)
-        for c in range(n_out):
-            fetch(c)
-            add_up(c)
-        for c in range(n_out):
-            take_log(c)
-            hand_on(c)
             if c >= n_out - 2:
-                part = slice(0 if c == n_out - 2 else o_spans[c][0], o_spans[c][0] + o_spans[c][1])
+                part = slice(0, cols.stop) if c == n_out - 2 else cols
                 nc.sync.dma_start(out_words[:, part], o_words[:, part].bitcast(I32))
         for q in range(QUADS):
-            engine = nc.scalar if q % 2 else nc.sync
-            engine.dma_start(
-                out_2[0, 4 * q : 4 * q + 4, :].bitcast(I32), o_scales[32 * q : 32 * q + 4, :].bitcast(I32)
-            )
+            queue = nc.scalar if q % 2 else nc.sync
+            queue.dma_start(out_2[0, 4 * q : 4 * q + 4, :].bitcast(I32), o_scales[32 * q : 32 * q + 4, :].bitcast(I32))

from contextlib import ExitStack

import concourse.mybir as mybir

K, T, S, N, H = 512, 2048, 512, 512, 512
FLOPS = 2 * S * (K * H + H * N + K * N)

F32 = mybir.dt.float32
BF16 = mybir.dt.bfloat16
I32 = mybir.dt.int32
U32 = mybir.dt.uint32
U16 = mybir.dt.uint16
U8 = mybir.dt.uint8
FP8X4 = mybir.dt.float8_e4m3fn_x4
FP4X4 = mybir.dt.float4_e2m1fn_x4
ALU = mybir.AluOpType
ACT = mybir.ActivationFunctionType

P = 128
PACK = 4
QUADS = 4
GROUP = 16
MEMBERS = 4
SPARE = 16
Z_WIDTHS = (256, 128, 128)
VECTOR_N2_TILES = 3
OUT_WIDTH = 128


def entries_of(first, last):
    return slice(first // GROUP, last // GROUP)


def tile_picked_mixingmaxglse_none_po_kernel(
    tc, x_words, x_scales, w1_words, w1_scales, gn, w2_words, w2_scales, w3_words, w3_scales,
    offs, n1, n2, two, n3, out_0, out_1, out_2,
):
    nc = tc.nc

    with ExitStack() as ctx:
        keep = ctx.enter_context(tc.tile_pool(name="keep", bufs=1))
        psum = ctx.enter_context(tc.psum_pool(name="psum", bufs=1))

        def load_list(src, name):
            tile = keep.tile(list(src.shape), U16, name=name)
            nc.sync.dma_start(tile[:], src)
            return tile

        def load_scale_rows(queues, plane, src):
            for q in range(QUADS):
                queues[q].dma_start(plane[32 * q : 32 * q + 4, :].bitcast(I32), src[0, 4 * q : 4 * q + 4, :].bitcast(I32))

        def load_words(queue, src, name, slot):
            raw = keep.tile([P, 2 * N], U8, name=name, tag=slot)
            queue.dma_start(raw[:].bitcast(I32), src[0].bitcast(I32))
            return raw

        def zeroed_plane(engine, width, name):
            plane = keep.tile([P, width], U8, name=name)
            engine.memset(plane[:].bitcast(I32), 0)
            return plane

        def deal(raw_words, raw_scales, name, slot):
            words = keep.tile([P, 2 * N], U8, name=name + "_words", tag=slot + "_words", align_bytes=64)
            scales = keep.tile([P, N], U8, name=name + "_scales", tag=slot + "_scales", align_bytes=64)
            nc.vector.tensor_copy(
                out=words[:].bitcast(U16).rearrange("p (t m) -> p t m", t=PACK),
                in_=raw_words[:].bitcast(U16).rearrange("p (m t) -> p t m", t=PACK),
            )
            nc.gpsimd.tensor_copy(
                out=scales[:].rearrange("p (t m) -> p t m", t=PACK),
                in_=raw_scales[:].rearrange("p (m t) -> p t m", t=PACK),
            )
            return words, scales

        def pick(lst, name, parts):
            words = keep.tile([P, S], U32, name=name + "_words", align_bytes=64)
            scales = keep.tile([P, S], U8, name=name + "_scales", align_bytes=64)
            nc.vector.tensor_copy(scales[:], x_plane[:].indirect(lst[:]))
            for part in parts:
                picked = x_table[:].bitcast(U32).indirect(lst[:, entries_of(part.start, part.stop)])
                nc.vector.tensor_copy(words[:, part], picked)
            return words, scales

        def product(bank, bank_cols, weights, t, moving, moving_cols, start, stop):
            nc.tensor.matmul_mx(
                out=bank[:, bank_cols],
                lhsT=weights[0][:, 2 * P * t : 2 * P * (t + 1)].bitcast(FP4X4),
                lhsT_scale=weights[1][:, P * t : P * (t + 1)],
                rhs=moving[0][:, moving_cols].bitcast(FP8X4),
                rhs_scale=moving[1][:, moving_cols],
                start=start,
                stop=stop,
            )

        w_plane = zeroed_plane(nc.gpsimd, H, "w_plane")
        x_plane = zeroed_plane(nc.vector, T, "x_plane")
        x_rows = keep.tile([P, T], U8, name="x_rows")
        load_scale_rows([nc.sync, nc.scalar] * 2, x_rows, x_scales)
        offs_t = load_list(offs, "offs_t")
        w1_raw = load_words(nc.scalar, w1_words, "w1_raw", "raw_first")
        x_table = keep.tile([P, T], I32, name="x_table")
        nc.sync.dma_start(x_table[:], x_words[0].rearrange("p n t -> p (n t)").bitcast(I32))
        load_scale_rows([nc.scalar, nc.sync] * 2, w_plane, w1_scales)
        gain = keep.tile([P, PACK], F32, name="gain")
        nc.scalar.dma_start(gain[:], gn.rearrange("(p t) o -> p (t o)", t=PACK))
        warm = keep.tile([P, 1], F32, name="warm")
        nc.scalar.activation(warm[:], gain[:, 0:1], ACT.Sigmoid)
        two_t = load_list(two, "two_t")
        n1_t = load_list(n1, "n1_t")
        n2_t = load_list(n2, "n2_t")
        w3_plane = zeroed_plane(nc.vector, N, "w3_plane")
        w3_raw = load_words(nc.sync, w3_words, "w3_raw", "raw_second")
        load_scale_rows([nc.sync] * QUADS, w3_plane, w3_scales)
        n3_t = load_list(n3, "n3_t")
        for q in range(QUADS):
            rows = slice(32 * q, 32 * q + 4)
            nc.vector.tensor_copy(x_plane[rows, :].bitcast(I32), x_rows[rows, :].bitcast(I32))

        ex = [keep.tile([P, S + SPARE], F32, name="ex%d" % t) for t in range(PACK)]
        for t in range(PACK):
            nc.vector.memset(ex[t][:, S:], 0.0)

        every = slice(0, S)
        halves = [slice(0, S // 2), slice(S // 2, S)]
        z_starts = [sum(Z_WIDTHS[:c]) for c in range(len(Z_WIDTHS))]
        stretches = [slice(c0, c0 + cw) for c0, cw in zip(z_starts, Z_WIDTHS)]
        split, late_width = z_starts[-1], Z_WIDTHS[-1]
        w1 = deal(w1_raw, w_plane, "w1", "token_side")
        w2_raw = load_words(nc.sync, w2_words, "w2_raw", "raw_first")
        load_scale_rows([nc.sync] * QUADS, w_plane, w2_scales)
        x_one = pick(offs_t, "x_one", halves)
        y_bank = [psum.tile([P, S], F32, name="y_bank%d" % t, tag="bank%d" % t) for t in range(PACK)]
        h_bank = [psum.tile([P, S], F32, name="h_bank%d" % t) for t in range(PACK)]
        y = [keep.tile([P, S], F32, name="y%d" % t) for t in range(PACK)]
        for t in range(PACK):
            for half in halves:
                product(y_bank[t], half, w1, t, x_one, half, True, True)
        nc.scalar.activation(y[0][:], y_bank[0][:], ACT.Copy)

        x_two = pick(two_t, "x_two", [every])
        w3 = deal(w3_raw, w3_plane, "w3", "token_side")
        for t in range(PACK):
            for c, cols in enumerate(stretches[:-1]):
                product(h_bank[t], cols, w3, t, x_two, cols, c == 0, False)
        w2 = deal(w2_raw, w_plane, "w2", "hidden_side")

        for c, cols in enumerate(stretches):
            cw = Z_WIDTHS[c]
            late = cols.start == split
            entries = entries_of(cols.start, cols.stop)
            gate = keep.tile([P, PACK, cw], F32, name="gate%d" % c)
            other = keep.tile([P, PACK, cw], F32, name="other%d" % c)
            gated = keep.tile([P, PACK, cw], F32, name="gated%d" % c)
            larger = keep.tile([P, PACK, cw], F32, name="larger%d" % c, tag="larger_last" if late else "larger%d" % c)
            z_bf = keep.tile([P, cw, PACK], BF16, name="z_bf%d" % c, align_bytes=64)
            z_words = keep.tile([P, cw], U32, name="z_words%d" % c, align_bytes=64)
            z_scales = keep.tile([P, cw], U8, name="z_scales%d" % c, align_bytes=64)
            for t in range(PACK):
                if c == 0 and t + 1 < PACK:
                    nc.scalar.activation(y[t + 1][:], y_bank[t + 1][:], ACT.Copy)
                nc.scalar.activation(gate[:, t, :], y[t][:].indirect(n1_t[:, entries]), ACT.Sigmoid)
                if c == 0 and t < VECTOR_N2_TILES:
                    nc.vector.tensor_copy(other[:, t, :], y[t][:].indirect(n2_t[:, entries]))
                else:
                    nc.scalar.activation(other[:, t, :], y[t][:].indirect(n2_t[:, entries]), ACT.Copy)
                nc.vector.tensor_tensor(gated[:, t, :], gate[:, t, :], y_bank[t][:, cols], ALU.mult)
                if t % 2 == 1:
                    pair = slice(t - 1, t + 1)
                    nc.vector.tensor_tensor(larger[:, pair, :], gated[:, pair, :], other[:, pair, :], ALU.max)
            if late:
                late_bank = [psum.tile([P, S], F32, name="late_bank%d" % t, tag="bank%d" % t) for t in range(PACK)]
                for t in range(PACK):
                    product(late_bank[t], slice(0, cw), w3, t, x_two, cols, True, False)
            nc.vector.tensor_tensor(
                z_bf[:].rearrange("p (c i) t -> p c t i", i=2),
                larger[:].rearrange("p t (c i) -> p c t i", i=2),
                gain[:].unsqueeze(1).unsqueeze(3).to_broadcast([P, cw // 2, PACK, 2]),
                ALU.mult,
            )
            nc.vector.quantize_mx(
                out=z_words[:].bitcast(FP8X4), scales=z_scales[:], in_=z_bf[:].rearrange("p c t -> p (c t)")
            )
            for t in range(PACK):
                if late:
                    product(late_bank[t], slice(0, cw), w2, t, (z_words, z_scales), slice(0, cw), False, True)
                else:
                    product(h_bank[t], cols, w2, t, (z_words, z_scales), slice(0, cw), False, cols.stop == split)

        inverse = keep.tile([P, PACK, S], F32, name="inverse", tag="larger_last")
        for t in range(PACK):
            nc.scalar.activation(ex[t][:, :split], h_bank[t][:, :split], ACT.Exp)
            nc.scalar.activation(ex[t][:, split:S], late_bank[t][:, :late_width], ACT.Exp)
        for t in range(PACK):
            nc.scalar.activation(inverse[:, t, :split], h_bank[t][:, :split], ACT.Exp, scale=-1.0)
            nc.scalar.activation(inverse[:, t, split:], late_bank[t][:, :late_width], ACT.Exp, scale=-1.0)

        n_out = S // OUT_WIDTH
        out_cols = [slice(c * OUT_WIDTH, (c + 1) * OUT_WIDTH) for c in range(n_out)]
        o_words = keep.tile([P, S], U32, name="o_words", align_bytes=64)
        o_scales = keep.tile([P, S], U8, name="o_scales", align_bytes=64)
        ratio = []
        for c, cols in enumerate(out_cols):
            entries = entries_of(MEMBERS * cols.start, MEMBERS * cols.stop)
            members = [keep.tile([P, 2, MEMBERS * OUT_WIDTH], F32, name="members%d_%d" % (c, u)) for u in range(2)]
            for t in range(PACK):
                fetched = ex[t][:].indirect(n3_t[:, entries])
                if c == 0 or t == PACK - 1:
                    nc.vector.tensor_copy(members[t // 2][:, t % 2, :], fetched)
                else:
                    nc.scalar.activation(members[t // 2][:, t % 2, :], fetched, ACT.Copy)
            pairs = keep.tile([P, PACK, OUT_WIDTH, 2], F32, name="pairs%d" % c)
            sums = keep.tile([P, PACK, OUT_WIDTH], F32, name="sums%d" % c)
            ratio.append(keep.tile([P, PACK, OUT_WIDTH], F32, name="ratio%d" % c))
            for u in range(2):
                four = members[u][:].rearrange("p t (j m) -> p (t j) m", m=MEMBERS)
                nc.vector.tensor_tensor(
                    pairs[:, 2 * u : 2 * u + 2, :, :].rearrange("p t j e -> p (t j) e"), four[:, :, 0:2], four[:, :, 2:4], ALU.add
                )
            nc.vector.tensor_tensor(sums[:], pairs[:, :, :, 0], pairs[:, :, :, 1], ALU.add)
            nc.vector.tensor_tensor(ratio[c][:], sums[:], inverse[:, :, cols], ALU.mult)

        out_rows = out_0.rearrange("(p t) j -> p t j", t=PACK)
        out_words = out_1[0].rearrange("p n t -> p (n t)").bitcast(I32)
        for c, cols in enumerate(out_cols):
            result = keep.tile([P, PACK, OUT_WIDTH], F32, name="result%d" % c)
            nc.scalar.activation(result[:], ratio[c][:], ACT.Ln, bias=1.0)
            nc.sync.dma_start(out_rows[:, :, cols], result[:])
            o_bf = keep.tile([P, OUT_WIDTH, PACK], BF16, name="o_bf%d" % c, align_bytes=64)
            nc.vector.tensor_copy(
                out=o_bf[:].rearrange("p (c i) t -> p c t i", i=4),
                in_=result[:].rearrange("p t (c i) -> p c t i", i=4),
            )
            nc.vector.quantize_mx(
                out=o_words[:, cols].bitcast(FP8X4),
                scales=o_scales[:, cols],
                in_=o_bf[:].rearrange("p c t -> p (c t)"),
            )
            if c >= n_out - 2:
                part = slice(0, cols.stop) if c == n_out - 2 else cols
                nc.sync.dma_start(out_words[:, part], o_words[:, part].bitcast(I32))
        for q in range(QUADS):
            queue = nc.scalar if q % 2 else nc.sync
            queue.dma_start(out_2[0, 4 * q : 4 * q + 4, :].bitcast(I32), o_scales[32 * q : 32 * q + 4, :].bitcast(I32))
